import numpy as np
import ml_dtypes


def mxq(x, axis, fmt="e4m3"):
    dtype, down = {"e4m3": (ml_dtypes.float8_e4m3fn, 7), "e5m2": (ml_dtypes.float8_e5m2, 14)}[fmt]
    v = np.moveaxis(np.asarray(x, np.float32).astype(ml_dtypes.bfloat16).astype(np.float64), axis, -1)
    blocks = v.reshape(v.shape[:-1] + (-1, 32))
    amax = np.abs(blocks).max(-1, keepdims=True)
    byte = np.maximum(np.where(amax > 0, np.frexp(amax)[1] - 1 + 127, 0) - down, 1)
    scale = np.exp2(byte - 127.0)
    codes = (blocks / scale).astype(np.float32).astype(dtype).astype(np.float64)
    return np.moveaxis((codes * scale).reshape(v.shape), -1, axis)


WIDE = False


def mx_kscale(k):
    if not WIDE:
        return np.ones(k)
    levels = np.array([10, -10, 5, -5, 0])
    if k % 512:
        return np.exp2(np.random.permutation(np.resize(levels, k // 32))).repeat(32)
    a = np.empty((k // 512, 16))
    for p in range(k // 512):
        a[p, :8] = np.random.permutation(np.resize(levels, 8))
        for g in range(8):
            far = levels[np.abs(levels - a[p, g]) >= 10]
            a[p, g + 8] = far[np.random.randint(len(far))]
    return np.exp2(a.ravel()).repeat(32)


BF16 = ml_dtypes.bfloat16


def bf(x):
    return np.asarray(x, np.float32).astype(BF16)


def f64(x):
    return np.asarray(x).astype(np.float64)


E2M1 = np.array([0.0, 0.5, 1.0, 1.5, 2.0, 3.0, 4.0, 6.0, -0.0, -0.5, -1.0, -1.5, -2.0, -3.0, -4.0, -6.0])


def pack_weight(w, fmt):
    k, n = w.shape
    w = f64(bf(w)).reshape(k // 32, 32, n)
    amax = np.abs(w).max(1)
    if fmt == "e4m3":
        byte = np.frexp(amax)[1] - 1 + 127 - 7
    else:
        mant, ex = np.frexp(amax / 6.0)
        byte = np.where(mant > 0.5, ex, ex - 1) + 127
    byte = np.clip(np.where(amax > 0, byte, 1), 1, 254)
    scaled = (w * np.exp2(127.0 - byte)[:, None, :]).reshape(k, n).astype(np.float32)
    by_word = np.ascontiguousarray(scaled.reshape(k // 512, 128, 4, n).transpose(0, 1, 3, 2))
    if fmt == "e4m3":
        words = by_word.astype(ml_dtypes.float8_e4m3fn).view(np.uint8)
    else:
        c = by_word.astype(ml_dtypes.float4_e2m1fn).view(np.uint8) & 0xF
        words = c[..., 0::2] | (c[..., 1::2] << 4)
    return np.ascontiguousarray(words), np.ascontiguousarray(byte.astype(np.uint8).reshape(k // 512, 16, n))


def unpack_weight(words, scales, fmt):
    g, p, n, _ = words.shape
    if fmt == "e4m3":
        vals = np.ascontiguousarray(words).view(ml_dtypes.float8_e4m3fn).astype(np.float64)
    else:
        nib = np.empty((g, p, n, 4), np.uint8)
        nib[..., 0::2] = words & 0xF
        nib[..., 1::2] = words >> 4
        vals = E2M1[nib]
    vals = vals * np.repeat(np.exp2(scales.astype(np.float64) - 127.0), 8, axis=1)[..., None]
    return vals.transpose(0, 1, 3, 2).reshape(g * 512, n)
def pack4(w):
    words, scales = pack_weight(w, "e2m1")
    return words.reshape(words.shape[0], 128, -1), scales


def unpack4(words, scales):
    return unpack_weight(words.reshape(words.shape[0], 128, -1, 2), scales, "e2m1")


def planes(Y):
    n, m = Y.shape
    b = f64(bf(Y)).reshape(n // 32, 32, m)
    amax = np.abs(b).max(1)
    byte = np.clip(np.where(amax > 0, np.frexp(amax)[1] - 1 + 127 - 7, 1), 1, 254)
    codes = (b * np.exp2(127.0 - byte)[:, None, :]).reshape(n, m).astype(np.float32).astype(ml_dtypes.float8_e4m3fn).view(np.uint8)
    words = codes.reshape(n // 512, 128, 4, m).transpose(0, 1, 3, 2)
    return np.ascontiguousarray(words), np.ascontiguousarray(byte.astype(np.uint8).reshape(n // 512, 16, m))


P, S = 1024, 1536

LOW, HIGH = -0.5, 1.5


def setup_inputs():
    s = mx_kscale(S)
    t = mx_kscale(P)
    x = 0.5 * np.exp(np.random.randn(P, S)) * s[None, :] * t[:, None]
    x_words, x_scales = pack_weight(x.T, "e4m3")
    a = np.random.randn(S, S) / np.sqrt(S) / s[:, None]
    a_words, a_scales = pack4(a)
    growth = 0.5 * np.exp(0.5 * np.random.randn(P, S)) * t[:, None]
    w = np.exp(1.8 * np.random.randn(P, P))
    dispersal = w / w.sum(axis=1, keepdims=True) / t[None, :]
    habitat = np.exp(0.7 * np.random.randn(1, S) + 0.2 * np.random.randn(P, S))
    return {"x_words": x_words, "x_scales": x_scales, "a_words": a_words, "a_scales": a_scales,
            "growth": bf(growth), "dispersal": bf(dispersal), "habitat": bf(habitat)}


def reference(x_words, x_scales, a_words, a_scales, growth, dispersal, habitat):
    x = unpack_weight(x_words, x_scales, "e4m3").T
    a = unpack4(a_words, a_scales)
    h = (x @ a) + f64(growth)
    hq = mxq(h, 0, "e4m3")
    dq = mxq(f64(dispersal), 1, "e4m3")
    v = dq @ hq
    y = np.minimum(np.maximum(v, LOW), HIGH) * f64(habitat)
    words, scales = planes(y.T)
    return y, words, scales

@@ -1,0 +1,354 @@
+from contextlib import ExitStack
+
+import concourse.mybir as mybir
+from concourse.masks import make_identity
+
+PATCHES, SPECIES = 1024, 1536
+LOW, HIGH = -0.5, 1.5
+FLOPS = 2 * PATCHES * SPECIES * SPECIES + 2 * PATCHES * PATCHES * SPECIES
+
+F32 = mybir.dt.float32
+BF16 = mybir.dt.bfloat16
+I32 = mybir.dt.int32
+U8 = mybir.dt.uint8
+FP8X4 = mybir.dt.float8_e4m3fn_x4
+FP4X4 = mybir.dt.float4_e2m1fn_x4
+ALU = mybir.AluOpType
+
+P = 128
+PACK = 4
+GROUP = P * PACK
+S_GROUPS = SPECIES // GROUP
+P_GROUPS = PATCHES // GROUP
+STRIP = 256
+STRIPS = SPECIES // STRIP
+PAIRS = PATCHES // (2 * P)
+UNITS = STRIPS * PAIRS
+LAG = 5
+RUN = 4
+DIRECT = (19, 21, 23)
+
+
+def tile_dispersed_species_growth_h2_kernel(
+    tc, x_words, x_scales, a_words, a_scales, growth, dispersal, habitat, out_0, out_1, out_2
+):
+    nc = tc.nc
+    with ExitStack() as ctx:
+        keep = ctx.enter_context(tc.tile_pool(name="keep", bufs=1))
+        flow = ctx.enter_context(tc.tile_pool(name="flow", bufs=2))
+        h_psum = ctx.enter_context(tc.psum_pool(name="h_psum", bufs=3))
+        v_psum = ctx.enter_context(tc.psum_pool(name="v_psum", bufs=3))
+        t_psum = ctx.enter_context(tc.psum_pool(name="t_psum", bufs=2))
+        ctx.enter_context(tc.manual_schedule())
+
+        def kept(name, shape, dtype):
+            return keep.tile(shape, dtype, name=name, align_bytes=64)
+
+        def load_scale_rows(plane, scales, cols):
+            for quad in range(4):
+                nc.sync.dma_start(
+                    out=plane[32 * quad : 32 * quad + 4, :, :].bitcast(I32),
+                    in_=scales[:, 4 * quad : 4 * quad + 4, cols].rearrange("g r n -> r g n").bitcast(I32),
+                )
+
+        x_scale_raw = kept("x_scale_raw", [P, S_GROUPS, PATCHES], U8)
+        a_scale_first = kept("a_scale_first", [P, S_GROUPS, GROUP], U8)
+        a_scale_rest = kept("a_scale_rest", [P, S_GROUPS, SPECIES - GROUP], U8)
+        ident = kept("ident", [P, P], F32)
+        for plane in (x_scale_raw, a_scale_first, a_scale_rest):
+            nc.vector.memset(plane[:].bitcast(I32), 0)
+        nc.vector.memset(ident[:], 0.0)
+        make_identity(nc, ident[:], nomemset=True)
+
+        x_raw, a_code, grow, disp, hab = {}, {}, {}, {}, {}
+
+        def load_x(pg):
+            for sg in range(S_GROUPS):
+                x_raw[pg, sg] = kept("x_raw_%d_%d" % (pg, sg), [P, GROUP], I32)
+                row = x_words[sg].rearrange("p n t -> p (n t)")
+                nc.sync.dma_start(
+                    out=x_raw[pg, sg][:], in_=row[:, PACK * GROUP * pg : PACK * GROUP * (pg + 1)].bitcast(I32)
+                )
+
+        def load_a(first_strip, strips):
+            tile = kept("a_code_%d" % first_strip, [P, S_GROUPS, 2 * STRIP * strips], U8)
+            cols = slice(2 * STRIP * first_strip, 2 * STRIP * (first_strip + strips))
+            nc.sync.dma_start(
+                out=tile[:].bitcast(I32), in_=a_words[:, :, cols].rearrange("g p n -> p g n").bitcast(I32)
+            )
+            for s in range(strips):
+                a_code[first_strip + s] = tile[:, :, 2 * STRIP * s : 2 * STRIP * (s + 1)]
+
+        def load_growth(pg, first_strip, strips):
+            tile = kept("grow_%d_%d" % (pg, first_strip), [P, PACK, strips * STRIP], BF16)
+            cols = slice(first_strip * STRIP, (first_strip + strips) * STRIP)
+            nc.sync.dma_start(
+                out=tile[:], in_=growth[GROUP * pg : GROUP * (pg + 1), cols].rearrange("(p t) s -> p t s", t=PACK)
+            )
+            for s in range(strips):
+                grow[pg, first_strip + s] = tile[:, :, s * STRIP : (s + 1) * STRIP]
+
+        def load_dispersal(pair):
+            disp[pair] = kept("disp_%d" % pair, [P, 2, PATCHES], BF16)
+            nc.sync.dma_start(
+                out=disp[pair][:],
+                in_=dispersal[2 * P * pair : 2 * P * (pair + 1), :].rearrange("(j p) k -> p j k", p=P),
+            )
+
+        def load_habitat(c, half):
+            tile = kept("hab_%d_%d" % (c, half), [P, 4, GROUP], BF16)
+            nc.sync.dma_start(
+                out=tile[:],
+                in_=habitat[GROUP * half : GROUP * (half + 1), GROUP * c : GROUP * (c + 1)].rearrange(
+                    "(j p) s -> p j s", p=P
+                ),
+            )
+            for q in range(2):
+                for hh in range(2):
+                    hab[2 * c + hh, 2 * half + q] = tile[:, 2 * q : 2 * q + 2, STRIP * hh : STRIP * (hh + 1)]
+
+        load_x(0)
+        load_scale_rows(x_scale_raw, x_scales, slice(0, PATCHES))
+        load_scale_rows(a_scale_first, a_scales, slice(0, GROUP))
+        load_a(0, 1)
+        load_x(1)
+        load_growth(0, 0, 1)
+        load_growth(1, 0, 1)
+        load_dispersal(0)
+        load_a(1, 1)
+        load_dispersal(1)
+        load_growth(0, 1, 1)
+        load_dispersal(2)
+        load_growth(1, 1, 1)
+        load_dispersal(3)
+        load_habitat(0, 0)
+        load_habitat(0, 1)
+        load_scale_rows(a_scale_rest, a_scales, slice(GROUP, SPECIES))
+        for c in range(1, S_GROUPS):
+            load_a(2 * c, 2)
+            load_growth(0, 2 * c, 2)
+            load_growth(1, 2 * c, 2)
+            load_habitat(c, 0)
+            load_habitat(c, 1)
+
+        x_code, x_scale = {}, {}
+
+        def order_x_words(pg):
+            for sg in range(S_GROUPS):
+                x_code[pg, sg] = kept("x_code_%d_%d" % (pg, sg), [P, GROUP], I32)
+                nc.vector.tensor_copy(
+                    out=x_code[pg, sg][:].rearrange("p (t m) -> p m t", t=PACK),
+                    in_=x_raw[pg, sg][:].rearrange("p (m t) -> p m t", t=PACK),
+                )
+
+        def order_x_scales(pg, first_t, count):
+            tile = kept("x_scale_%d_%d" % (pg, first_t), [P, count, S_GROUPS, P], U8)
+            raw = x_scale_raw[:, :, GROUP * pg : GROUP * (pg + 1)].rearrange("p g (m t) -> p t g m", t=PACK)
+            nc.vector.tensor_copy(out=tile[:], in_=raw[:, first_t : first_t + count])
+            for t in range(count):
+                x_scale[pg, first_t + t] = tile[:, t]
+
+        order_x_words(0)
+        order_x_scales(0, 0, 2)
+        order_x_scales(0, 2, 2)
+        order_x_scales(1, 0, 4)
+        order_x_words(1)
+
+        h_bank, h_bf, h_code, h_scale = {}, {}, {}, {}
+        d_bank, d_bf, d_code, d_scale = {}, {}, {}, {}
+        v_bank, y, y_bf = {}, {}, {}
+        yt_bank, yt_bf = {}, {}
+        y_code = [kept("y_code_%d" % g, [P, PATCHES], I32) for g in range(S_GROUPS)]
+        y_scale = [kept("y_scale_%d" % g, [P, PATCHES], U8) for g in range(S_GROUPS)]
+
+        def interactions(k):
+            strip, pg, b = k // 4, k // 2 % 2, k % 2
+            c, first = divmod(strip * STRIP + b * P, GROUP)
+            if c == 0:
+                a_plane, scale_first = a_scale_first, first
+            else:
+                a_plane, scale_first = a_scale_rest, first + (c - 1) * GROUP
+            h_bank[k] = h_psum.tile([P, PACK, P], F32, name="h_bank")
+            for t in range(PACK):
+                cols = slice(P * t, P * (t + 1))
+                for sg in range(S_GROUPS):
+                    nc.tensor.matmul_mx(
+                        out=h_bank[k][:, t, :],
+                        lhsT=x_code[pg, sg][:, cols].bitcast(FP8X4),
+                        lhsT_scale=x_scale[pg, t][:, sg, :],
+                        rhs=a_code[strip][:, sg, 2 * P * b : 2 * P * (b + 1)].bitcast(FP4X4),
+                        rhs_scale=a_plane[:, sg, scale_first : scale_first + P],
+                        start=(sg == 0),
+                        stop=(sg == S_GROUPS - 1),
+                    )
+
+        def add_growth(k):
+            strip, pg, b = k // 4, k // 2 % 2, k % 2
+            if b == 0:
+                h_bf[strip, pg] = flow.tile([P, STRIP, PACK], BF16, name="h_bf", bufs=3, align_bytes=64)
+            nc.vector.tensor_tensor(
+                out=h_bf[strip, pg][:, P * b : P * (b + 1), :].rearrange("p (c i) t -> p c t i", i=RUN),
+                in0=h_bank[k][:].rearrange("p t (c i) -> p c t i", i=RUN),
+                in1=grow[pg, strip][:, :, P * b : P * (b + 1)].rearrange("p t (c i) -> p c t i", i=RUN),
+                op=ALU.add,
+            )
+
+        def quantize_h(strip, pg):
+            h_code[strip, pg] = kept("h_code_%d_%d" % (strip, pg), [P, STRIP], I32)
+            h_scale[strip, pg] = kept("h_scale_%d_%d" % (strip, pg), [P, STRIP], U8)
+            nc.vector.quantize_mx(
+                out=h_code[strip, pg][:].bitcast(FP8X4),
+                scales=h_scale[strip, pg][:],
+                in_=h_bf[strip, pg][:].rearrange("p n t -> p (n t)"),
+            )
+
+        def transpose_dispersal(pair):
+            for j in range(2):
+                words = disp[pair][:, j, :].bitcast(F32)
+                d_bank[pair, j] = t_psum.tile([P, P_GROUPS, 2, P], F32, name="t_bank")
+                for pg in range(P_GROUPS):
+                    for u in range(2):
+                        nc.tensor.transpose(
+                            d_bank[pair, j][:, pg, u, :], words[:, 2 * P * pg + u : 2 * P * (pg + 1) : 2], ident[:]
+                        )
+
+        def unload_dispersal(pair):
+            d_bf[pair] = flow.tile([P, 2, P_GROUPS * P * PACK], BF16, name="d_bf", bufs=2, align_bytes=64)
+            for j in range(2):
+                nc.scalar.copy(
+                    out=d_bf[pair][:, j, :].bitcast(F32).rearrange("p (g r u) -> p g r u", g=P_GROUPS, u=2),
+                    in_=d_bank[pair, j][:].rearrange("p g u r -> p g r u"),
+                )
+
+        def quantize_dispersal(pair):
+            d_code[pair] = kept("d_code_%d" % pair, [P, 2 * P_GROUPS * P], I32)
+            d_scale[pair] = kept("d_scale_%d" % pair, [P, 2 * P_GROUPS * P], U8)
+            nc.vector.quantize_mx(
+                out=d_code[pair][:].bitcast(FP8X4),
+                scales=d_scale[pair][:],
+                in_=d_bf[pair][:].rearrange("p j n -> p (j n)"),
+            )
+
+        def mix(i):
+            strip, pair = divmod(i, PAIRS)
+            v_bank[i] = v_psum.tile([P, 2, STRIP], F32, name="v_bank")
+            for j in range(2):
+                for pg in range(P_GROUPS):
+                    cols = slice(P * (P_GROUPS * j + pg), P * (P_GROUPS * j + pg + 1))
+                    nc.tensor.matmul_mx(
+                        out=v_bank[i][:, j, :],
+                        lhsT=d_code[pair][:, cols].bitcast(FP8X4),
+                        lhsT_scale=d_scale[pair][:, cols],
+                        rhs=h_code[strip, pg][:].bitcast(FP8X4),
+                        rhs_scale=h_scale[strip, pg][:],
+                        start=(pg == 0),
+                        stop=(pg == P_GROUPS - 1),
+                    )
+
+        def unload_mix(i):
+            y[i] = flow.tile([P, 2, STRIP], F32, name="y", bufs=14, align_bytes=64)
+            if i not in DIRECT:
+                nc.scalar.copy(out=y[i][:], in_=v_bank[i][:])
+
+        def clip(i):
+            source = v_bank[i] if i in DIRECT else y[i]
+            nc.vector.tensor_scalar(
+                out=y[i][:], in0=source[:], scalar1=LOW, scalar2=HIGH, op0=ALU.max, op1=ALU.min
+            )
+
+        def weigh(i):
+            strip, pair = divmod(i, PAIRS)
+            nc.vector.tensor_tensor(out=y[i][:], in0=y[i][:], in1=hab[strip, pair], op=ALU.mult)
+            nc.sync.dma_start(
+                out=out_0[2 * P * pair : 2 * P * (pair + 1), STRIP * strip : STRIP * (strip + 1)].rearrange(
+                    "(j p) s -> p j s", p=P
+                ),
+                in_=y[i][:],
+            )
+
+        def round_y(i):
+            strip, pair = divmod(i, PAIRS)
+            g, hh = divmod(strip, 2)
+            if hh == 0:
+                y_bf[g, pair] = flow.tile([P, 2, 2, STRIP], BF16, name="y_bf", bufs=8, align_bytes=64)
+            nc.scalar.copy(
+                out=y_bf[g, pair][:, :, :, P * hh : P * (hh + 1)].rearrange("p u j (m e) -> p u j m e", e=2),
+                in_=y[i][:].rearrange("p j (m u e) -> p u j m e", u=2, e=2),
+            )
+
+        def transpose_y(g, pair):
+            yt_bank[g, pair] = t_psum.tile([P, 2, 2, P], F32, name="t_bank")
+            for j in range(2):
+                for u in range(2):
+                    nc.tensor.transpose(yt_bank[g, pair][:, j, u, :], y_bf[g, pair][:, u, j, :].bitcast(F32), ident[:])
+
+        def unload_y(g, pair):
+            yt_bf[g, pair] = flow.tile([P, 2 * P * PACK], BF16, name="yt_bf", bufs=3, align_bytes=64)
+            nc.scalar.copy(
+                out=yt_bf[g, pair][:].bitcast(F32).rearrange("p (j r u) -> p j r u", j=2, u=2),
+                in_=yt_bank[g, pair][:].rearrange("p j u r -> p j r u"),
+            )
+
+        def quantize_y(g, pair):
+            cols = slice(2 * P * pair, 2 * P * (pair + 1))
+            nc.vector.quantize_mx(
+                out=y_code[g][:, cols].bitcast(FP8X4), scales=y_scale[g][:, cols], in_=yt_bf[g, pair][:]
+            )
+            last_group = g == S_GROUPS - 1
+            if last_group or pair % 2 == 1:
+                first = pair if last_group else pair - 1
+                cols = slice(2 * P * first, 2 * P * (pair + 1))
+                words = out_1[g].rearrange("p m t -> p (m t)").bitcast(I32)
+                nc.sync.dma_start(out=words[:, cols], in_=y_code[g][:, cols])
+            if pair == PAIRS - 1:
+                for quad in range(4):
+                    nc.sync.dma_start(
+                        out=out_2[g, 4 * quad : 4 * quad + 4, :].bitcast(I32),
+                        in_=y_scale[g][32 * quad : 32 * quad + 4, :].bitcast(I32),
+                    )
+
+        transpose_at, unload_at, quantize_at = {}, {}, {}
+        for g in range(S_GROUPS):
+            for pair in range(PAIRS):
+                rounded = LAG + 3 + 2 * PAIRS * g + PAIRS
+                if g == S_GROUPS - 1:
+                    turned = rounded + pair
+                    unloaded = turned + 1
+                    done = unloaded
+                else:
+                    turned = rounded + (pair | 1) + 1
+                    unloaded = turned + 1 + pair % 2
+                    done = unloaded + 1
+                transpose_at.setdefault(turned, []).append((g, pair))
+                unload_at.setdefault(unloaded, []).append((g, pair))
+                quantize_at.setdefault(done, []).append((g, pair))
+
+        for step in range(max(quantize_at) + 1):
+            i = step - LAG
+            if step < UNITS:
+                interactions(step)
+            if 0 <= i < UNITS:
+                mix(i)
+            if 0 <= i - 1 < UNITS:
+                unload_mix(i - 1)
+            if 0 <= step - 1 < UNITS:
+                add_growth(step - 1)
+            if 0 <= i - 2 < UNITS:
+                weigh(i - 2)
+            if 0 <= step - 1 < UNITS and step % 2 == 0:
+                quantize_h((step - 1) // 4, (step - 1) // 2 % 2)
+            if 0 <= i - 1 < UNITS:
+                clip(i - 1)
+            if 0 <= i - 3 < UNITS:
+                round_y(i - 3)
+            if 0 <= i + 1 < PAIRS:
+                unload_dispersal(i + 1)
+                quantize_dispersal(i + 1)
+            for g, pair in unload_at.get(step, []):
+                unload_y(g, pair)
+            for g, pair in quantize_at.get(step, []):
+                quantize_y(g, pair)
+            if 0 <= i + 2 < PAIRS:
+                transpose_dispersal(i + 2)
+            for g, pair in transpose_at.get(step, []):
+                transpose_y(g, pair)

@@ -24,9 +24,15 @@ STRIP = 256
 STRIPS = SPECIES // STRIP
 PAIRS = PATCHES // (2 * P)
 UNITS = STRIPS * PAIRS
-LAG = 5
+HALVES = PATCHES // GROUP
+ROUNDS = STRIPS * HALVES
+LAG = 2
 RUN = 4
-DIRECT = (19, 21, 23)
+POOL_COLS = 80
+LOADS = (("x", 0,), ("xs",), ("as", 0,), ("a", 0, 1,), ("d", 0,), ("x", 1,), ("g", 0, 0, 1,), ("d", 1,), ("g", 1, 0, 1,), ("a", 1, 1,), ("d", 2,), ("d", 3,), ("g", 0, 1, 1,), ("g", 1, 1, 1,), ("a", 2, 2,), ("h", 0, 2, 0,), ("as", 1,), ("h", 0, 2, 1,), ("g", 0, 2, 2,), ("as", 2,), ("g", 1, 2, 2,), ("a", 4, 2,), ("h", 2, 4, 0,), ("h", 2, 4, 1,), ("g", 0, 4, 2,), ("g", 1, 4, 2,))
+STEPS = (("late",), ("xw", 0,), ("xs", 0, 2, 2,), ("od", 1, "N",), ("od", 0, "S",), ("xs", 0, 0, 2,), ("xs", 1, 0, 4,), ("xw", 1,), ("s1", 0,), ("add", 0,), ("td", 0,), ("ud", 0, 0, "S",), ("s1", 2,), ("add", 1,), ("ud", 0, 1, "S",), ("qh", 0, 0,), ("add", 2,), ("td", 1,), ("add", 3,), ("ud", 1, 1, "S",), ("qd", 0,), ("od", 2, "V",), ("ud", 1, 0, "S",), ("s1", 4,), ("qd", 1,), ("td", 2,), ("qh", 0, 1,), ("mix", 1,), ("ud", 2, 0, "V",), ("od", 3, "S",), ("ud", 2, 1, "S",), ("add", 4,), ("mix", 0,), ("add", 5,), ("qd", 2,), ("um", 0,), ("td", 3,), ("s1", 6,), ("ud", 3, 0, "S",), ("ud", 3, 1, "V",), ("qh", 1, 0,), ("um", 1,), ("qd", 3,), ("mix", 3,), ("clip", 0, 0, 4,), ("mix", 2,), ("um", 3,), ("add", 6,), ("add", 7,), ("gw", 0, 0, 4,), ("qh", 1, 1,), ("um", 2,), ("w", 0, 0, 4,), ("s1", 8,), ("mix", 5,), ("clip", 1, 0, 4,), ("gw", 1, 0, 4,), ("mix", 4,), ("ry", 0, 0, 4, "S",), ("um", 5,), ("add", 8,), ("add", 9,), ("w", 1, 0, 4,), ("qh", 2, 0,), ("um", 4,), ("ry", 1, 0, 4, "S",), ("s1", 10,), ("mix", 7,), ("clip", 2, 0, 4,), ("mix", 6,), ("um", 7,), ("add", 10,), ("add", 11,), ("gw", 2, 0, 4,), ("qh", 2, 1,), ("um", 6,), ("w", 2, 0, 4,), ("s1", 12,), ("mix", 9,), ("clip", 3, 0, 4,), ("gw", 3, 0, 4,), ("mix", 8,), ("ry", 2, 0, 4, "S",), ("um", 9,), ("add", 12,), ("add", 13,), ("w", 3, 0, 4,), ("qh", 3, 0,), ("um", 8,), ("ry", 3, 0, 4, "S",), ("s1", 14,), ("mix", 11,), ("clip", 4, 0, 4,), ("mix", 10,), ("um", 11,), ("add", 14,), ("add", 15,), ("gw", 4, 0, 4,), ("qh", 3, 1,), ("ty", 0, 0, 2, 2,), ("ty", 0, 0, 0, 2,), ("um", 10,), ("w", 4, 0, 4,), ("s1", 16,), ("uy", 0, 0, 2, 2, "S",), ("uy", 0, 0, 0, 2, "S",), ("mix", 13,), ("clip", 5, 0, 4,), ("gw", 5, 0, 4,), ("qy", 0, 0, 0, 4,), ("mix", 12,), ("ry", 4, 0, 4, "S",), ("um", 13,), ("add", 16,), ("add", 17,), ("w", 5, 0, 4,), ("qh", 4, 0,), ("um", 12,), ("ry", 5, 0, 4, "S",), ("s1", 18,), ("mix", 15,), ("clip", 6, 0, 4,), ("mix", 14,), ("um", 15,), ("add", 18,), ("add", 19,), ("gw", 6, 0, 4,), ("qh", 4, 1,), ("ty", 0, 1, 2, 2,), ("ty", 0, 1, 0, 2,), ("um", 14,), ("w", 6, 0, 4,), ("s1", 20,), ("uy", 0, 1, 2, 2, "S",), ("uy", 0, 1, 0, 2, "S",), ("mix", 17,), ("clip", 7, 0, 4,), ("gw", 7, 0, 4,), ("qy", 0, 1, 0, 4,), ("mix", 16,), ("ry", 6, 0, 4, "S",), ("um", 17,), ("add", 20,), ("add", 21,), ("w", 7, 0, 4,), ("qh", 5, 0,), ("um", 16,), ("ry", 7, 0, 4, "S",), ("s1", 22,), ("clip", 8, 0, 4,), ("mix", 18,), ("gw", 8, 0, 4,), ("add", 22,), ("um", 18,), ("mix", 19,), ("ty", 1, 0, 2, 2,), ("add", 23,), ("ty", 1, 1, 2, 2,), ("clip", 9, 0, 2,), ("um", 19,), ("qh", 5, 1,), ("mix", 20,), ("w", 8, 0, 4,), ("uy", 1, 0, 2, 2, "S",), ("clip", 9, 2, 2,), ("mix", 21,), ("ty", 1, 0, 0, 2,), ("uy", 1, 1, 2, 2, "S",), ("ry", 8, 0, 4, "S",), ("um", 21,), ("dclip", 20,), ("w", 9, 2, 2,), ("w", 10, 0, 2,), ("w", 9, 0, 2,), ("clip", 10, 2, 2,), ("mix", 22,), ("uy", 1, 0, 0, 2, "S",), ("qy", 1, 0, 0, 4,), ("ty", 1, 1, 0, 2,), ("mix", 23,), ("dclip", 22,), ("ry", 10, 0, 2, "S",), ("uy", 1, 1, 0, 2, "S",), ("ry", 9, 0, 2, "S",), ("w", 10, 2, 2,), ("ty", 2, 0, 0, 2,), ("w", 11, 0, 2,), ("qy", 1, 1, 0, 4,), ("uy", 2, 0, 0, 2, "S",), ("dclip", 23,), ("ry", 10, 2, 2, "S",), ("ry", 11, 0, 2, "S",), ("ry", 9, 2, 2, "S",), ("qy", 2, 0, 0, 2,), ("ty", 2, 0, 2, 2,), ("ty", 2, 1, 0, 2,), ("uy", 2, 0, 2, 2, "S",), ("w", 11, 3, 1,), ("w", 11, 2, 1,), ("ry", 11, 3, 1, "V",), ("uy", 2, 1, 0, 2, "S",), ("ty", 2, 1, 3, 1,), ("uy", 2, 1, 3, 1, "S",), ("ry", 11, 2, 1, "V",), ("qy", 2, 0, 2, 2,), ("ty", 2, 1, 2, 1,), ("qy", 2, 1, 0, 2,), ("uy", 2, 1, 2, 1, "V",), ("qy", 2, 1, 3, 1,), ("qy", 2, 1, 2, 1,))
+EARLY = 4
+WIDE_STORES = 1
 
 
 def tile_dispersed_species_growth_h2_kernel(
@@ -36,8 +42,8 @@ def tile_dispersed_species_growth_h2_kernel(
     with ExitStack() as ctx:
         keep = ctx.enter_context(tc.tile_pool(name="keep", bufs=1))
         flow = ctx.enter_context(tc.tile_pool(name="flow", bufs=2))
-        h_psum = ctx.enter_context(tc.psum_pool(name="h_psum", bufs=3))
-        v_psum = ctx.enter_context(tc.psum_pool(name="v_psum", bufs=3))
+        h_psum = ctx.enter_context(tc.psum_pool(name="h_psum", bufs=4))
+        v_psum = ctx.enter_context(tc.psum_pool(name="v_psum", bufs=2))
         t_psum = ctx.enter_context(tc.psum_pool(name="t_psum", bufs=2))
         ctx.enter_context(tc.manual_schedule())
 
@@ -52,10 +58,9 @@ def tile_dispersed_species_growth_h2_kernel(
                 )
 
         x_scale_raw = kept("x_scale_raw", [P, S_GROUPS, PATCHES], U8)
-        a_scale_first = kept("a_scale_first", [P, S_GROUPS, GROUP], U8)
-        a_scale_rest = kept("a_scale_rest", [P, S_GROUPS, SPECIES - GROUP], U8)
+        a_scale = [kept("a_scale_%d" % c, [P, S_GROUPS, GROUP], U8) for c in range(S_GROUPS)]
         ident = kept("ident", [P, P], F32)
-        for plane in (x_scale_raw, a_scale_first, a_scale_rest):
+        for plane in [x_scale_raw] + a_scale:
             nc.vector.memset(plane[:].bitcast(I32), 0)
         nc.vector.memset(ident[:], 0.0)
         make_identity(nc, ident[:], nomemset=True)
@@ -95,41 +100,23 @@ def tile_dispersed_species_growth_h2_kernel(
                 in_=dispersal[2 * P * pair : 2 * P * (pair + 1), :].rearrange("(j p) k -> p j k", p=P),
             )
 
-        def load_habitat(c, half):
-            tile = kept("hab_%d_%d" % (c, half), [P, 4, GROUP], BF16)
+        def load_habitat(first_strip, strips, half):
+            tile = kept("hab_%d_%d" % (first_strip, half), [P, PACK, strips * STRIP], BF16)
+            cols = slice(first_strip * STRIP, (first_strip + strips) * STRIP)
             nc.sync.dma_start(
                 out=tile[:],
-                in_=habitat[GROUP * half : GROUP * (half + 1), GROUP * c : GROUP * (c + 1)].rearrange(
-                    "(j p) s -> p j s", p=P
-                ),
+                in_=habitat[GROUP * half : GROUP * (half + 1), cols].rearrange("(j p) s -> p j s", p=P),
             )
-            for q in range(2):
-                for hh in range(2):
-                    hab[2 * c + hh, 2 * half + q] = tile[:, 2 * q : 2 * q + 2, STRIP * hh : STRIP * (hh + 1)]
+            for s in range(strips):
+                hab[first_strip + s, half] = tile[:, :, s * STRIP : (s + 1) * STRIP]
 
-        load_x(0)
-        load_scale_rows(x_scale_raw, x_scales, slice(0, PATCHES))
-        load_scale_rows(a_scale_first, a_scales, slice(0, GROUP))
-        load_a(0, 1)
-        load_x(1)
-        load_growth(0, 0, 1)
-        load_growth(1, 0, 1)
-        load_dispersal(0)
-        load_a(1, 1)
-        load_dispersal(1)
-        load_growth(0, 1, 1)
-        load_dispersal(2)
-        load_growth(1, 1, 1)
-        load_dispersal(3)
-        load_habitat(0, 0)
-        load_habitat(0, 1)
-        load_scale_rows(a_scale_rest, a_scales, slice(GROUP, SPECIES))
-        for c in range(1, S_GROUPS):
-            load_a(2 * c, 2)
-            load_growth(0, 2 * c, 2)
-            load_growth(1, 2 * c, 2)
-            load_habitat(c, 0)
-            load_habitat(c, 1)
+        loaders = {"x": load_x, "xs": lambda: load_scale_rows(x_scale_raw, x_scales, slice(0, PATCHES)), "as": lambda c: load_scale_rows(a_scale[c], a_scales, slice(c * GROUP, (c + 1) * GROUP)), "a": load_a, "g": load_growth, "d": load_dispersal, "h": load_habitat}
+        for name, *args in LOADS[:EARLY]:
+            loaders[name](*args)
+
+        def late_loads():
+            for name, *args in LOADS[EARLY:]:
+                loaders[name](*args)
 
         x_code, x_scale = {}, {}
 
@@ -148,39 +135,32 @@ def tile_dispersed_species_growth_h2_kernel(
             for t in range(count):
                 x_scale[pg, first_t + t] = tile[:, t]
 
-        order_x_words(0)
-        order_x_scales(0, 0, 2)
-        order_x_scales(0, 2, 2)
-        order_x_scales(1, 0, 4)
-        order_x_words(1)
 
         h_bank, h_bf, h_code, h_scale = {}, {}, {}, {}
-        d_bank, d_bf, d_code, d_scale = {}, {}, {}, {}
+        d_words, d_bank, d_bf, d_code, d_scale = {}, {}, {}, {}, {}
         v_bank, y, y_bf = {}, {}, {}
-        yt_bank, yt_bf = {}, {}
+        yt_bank, yt_bf, done_cols = {}, {}, {}
         y_code = [kept("y_code_%d" % g, [P, PATCHES], I32) for g in range(S_GROUPS)]
         y_scale = [kept("y_scale_%d" % g, [P, PATCHES], U8) for g in range(S_GROUPS)]
 
         def interactions(k):
-            strip, pg, b = k // 4, k // 2 % 2, k % 2
-            c, first = divmod(strip * STRIP + b * P, GROUP)
-            if c == 0:
-                a_plane, scale_first = a_scale_first, first
-            else:
-                a_plane, scale_first = a_scale_rest, first + (c - 1) * GROUP
-            h_bank[k] = h_psum.tile([P, PACK, P], F32, name="h_bank")
+            strip, pg = k // 4, k // 2 % 2
+            c, first = divmod(strip * STRIP, GROUP)
+            for b in range(2):
+                h_bank[k + b] = h_psum.tile([P, PACK, P], F32, name="h_bank")
             for t in range(PACK):
                 cols = slice(P * t, P * (t + 1))
                 for sg in range(S_GROUPS):
-                    nc.tensor.matmul_mx(
-                        out=h_bank[k][:, t, :],
-                        lhsT=x_code[pg, sg][:, cols].bitcast(FP8X4),
-                        lhsT_scale=x_scale[pg, t][:, sg, :],
-                        rhs=a_code[strip][:, sg, 2 * P * b : 2 * P * (b + 1)].bitcast(FP4X4),
-                        rhs_scale=a_plane[:, sg, scale_first : scale_first + P],
-                        start=(sg == 0),
-                        stop=(sg == S_GROUPS - 1),
-                    )
+                    for b in range(2):
+                        nc.tensor.matmul_mx(
+                            out=h_bank[k + b][:, t, :],
+                            lhsT=x_code[pg, sg][:, cols].bitcast(FP8X4),
+                            lhsT_scale=x_scale[pg, t][:, sg, :],
+                            rhs=a_code[strip][:, sg, 2 * P * b : 2 * P * (b + 1)].bitcast(FP4X4),
+                            rhs_scale=a_scale[c][:, sg, first + P * b : first + P * (b + 1)],
+                            start=(sg == 0),
+                            stop=(sg == S_GROUPS - 1),
+                        )
 
         def add_growth(k):
             strip, pg, b = k // 4, k // 2 % 2, k % 2
@@ -202,23 +182,29 @@ def tile_dispersed_species_growth_h2_kernel(
                 in_=h_bf[strip, pg][:].rearrange("p n t -> p (n t)"),
             )
 
+        def order_dispersal(pair, eng):
+            if eng == "N":
+                return
+            d_words[pair] = flow.tile([P, 2 * P_GROUPS, 2, P], F32, name="d_words", bufs=2, align_bytes=64)
+            words = disp[pair][:].rearrange("p j k -> p (j k)").bitcast(F32)
+            (nc.vector.tensor_copy if eng == "V" else nc.scalar.copy)(out=d_words[pair][:], in_=words.rearrange("p (a m u) -> p a u m", m=P, u=2))
+
         def transpose_dispersal(pair):
             for j in range(2):
-                words = disp[pair][:, j, :].bitcast(F32)
                 d_bank[pair, j] = t_psum.tile([P, P_GROUPS, 2, P], F32, name="t_bank")
                 for pg in range(P_GROUPS):
                     for u in range(2):
                         nc.tensor.transpose(
-                            d_bank[pair, j][:, pg, u, :], words[:, 2 * P * pg + u : 2 * P * (pg + 1) : 2], ident[:]
+                            d_bank[pair, j][:, pg, u, :], d_words[pair][:, P_GROUPS * j + pg, u, :] if pair in d_words else disp[pair][:, j, :].bitcast(F32)[:, 2 * P * pg + u : 2 * P * (pg + 1) : 2], ident[:]
                         )
 
-        def unload_dispersal(pair):
-            d_bf[pair] = flow.tile([P, 2, P_GROUPS * P * PACK], BF16, name="d_bf", bufs=2, align_bytes=64)
-            for j in range(2):
-                nc.scalar.copy(
-                    out=d_bf[pair][:, j, :].bitcast(F32).rearrange("p (g r u) -> p g r u", g=P_GROUPS, u=2),
-                    in_=d_bank[pair, j][:].rearrange("p g u r -> p g r u"),
-                )
+        def unload_dispersal(pair, j, eng):
+            if pair not in d_bf:
+                d_bf[pair] = flow.tile([P, 2, P_GROUPS * P * PACK], BF16, name="yt_bf", bufs=2, align_bytes=64)
+            (nc.vector.tensor_copy if eng == "V" else nc.scalar.copy)(
+                out=d_bf[pair][:, j, :].bitcast(F32).rearrange("p (g r u) -> p g r u", g=P_GROUPS, u=2),
+                in_=d_bank[pair, j][:].rearrange("p g u r -> p g r u"),
+            )
 
         def quantize_dispersal(pair):
             d_code[pair] = kept("d_code_%d" % pair, [P, 2 * P_GROUPS * P], I32)
@@ -245,110 +231,122 @@ def tile_dispersed_species_growth_h2_kernel(
                         stop=(pg == P_GROUPS - 1),
                     )
 
-        def unload_mix(i):
-            y[i] = flow.tile([P, 2, STRIP], F32, name="y", bufs=14, align_bytes=64)
-            if i not in DIRECT:
-                nc.scalar.copy(out=y[i][:], in_=v_bank[i][:])
-
-        def clip(i):
-            source = v_bank[i] if i in DIRECT else y[i]
-            nc.vector.tensor_scalar(
-                out=y[i][:], in0=source[:], scalar1=LOW, scalar2=HIGH, op0=ALU.max, op1=ALU.min
-            )
-
-        def weigh(i):
-            strip, pair = divmod(i, PAIRS)
-            nc.vector.tensor_tensor(out=y[i][:], in0=y[i][:], in1=hab[strip, pair], op=ALU.mult)
-            nc.sync.dma_start(
-                out=out_0[2 * P * pair : 2 * P * (pair + 1), STRIP * strip : STRIP * (strip + 1)].rearrange(
-                    "(j p) s -> p j s", p=P
-                ),
-                in_=y[i][:],
-            )
-
-        def round_y(i):
-            strip, pair = divmod(i, PAIRS)
+        def y_rows(q, first, count):
+            strip, half = divmod(q, HALVES)
             g, hh = divmod(strip, 2)
-            if hh == 0:
-                y_bf[g, pair] = flow.tile([P, 2, 2, STRIP], BF16, name="y_bf", bufs=8, align_bytes=64)
-            nc.scalar.copy(
-                out=y_bf[g, pair][:, :, :, P * hh : P * (hh + 1)].rearrange("p u j (m e) -> p u j m e", e=2),
-                in_=y[i][:].rearrange("p j (m u e) -> p u j m e", u=2, e=2),
+            if g >= WIDE_STORES:
+                if q not in y:
+                    y[q] = kept("y_%d" % q, [P, PACK, STRIP], F32)
+                return y[q][:, first : first + count, :]
+            if (g, half) not in y:
+                y[g, half] = kept("y_%d_%d" % (g, half), [P, PACK, GROUP], F32)
+            return y[g, half][:, first : first + count, STRIP * hh : STRIP * (hh + 1)]
+
+        def unload_mix(i):
+            nc.scalar.copy(out=y_rows(i // 2, 2 * (i % 2), 2), in_=v_bank[i][:])
+
+        def clip(q, first=0, count=4, source=None):
+            rows = y_rows(q, first, count)
+            nc.vector.tensor_scalar(
+                out=rows, in0=rows if source is None else source, scalar1=LOW, scalar2=HIGH, op0=ALU.max, op1=ALU.min
             )
 
-        def transpose_y(g, pair):
-            yt_bank[g, pair] = t_psum.tile([P, 2, 2, P], F32, name="t_bank")
-            for j in range(2):
+        def weigh(engine, q, cols, first=0, count=4):
+            strip, half = divmod(q, HALVES)
+            rows = y_rows(q, first, count)[:, :, cols]
+            engine.tensor_tensor(out=rows, in0=rows, in1=hab[strip, half][:, first : first + count, cols], op=ALU.mult)
+
+        def store_y(q, first=0, count=4):
+            strip, half = divmod(q, HALVES)
+            g, hh = divmod(strip, 2)
+            rows = slice(GROUP * half + P * first, GROUP * half + P * (first + count))
+            if g >= WIDE_STORES:
+                nc.sync.dma_start(
+                    out=out_0[rows, STRIP * strip : STRIP * (strip + 1)].rearrange("(j p) s -> p j s", p=P),
+                    in_=y_rows(q, first, count),
+                )
+            elif hh == 1:
+                nc.sync.dma_start(
+                    out=out_0[rows, GROUP * g : GROUP * (g + 1)].rearrange("(j p) s -> p j s", p=P),
+                    in_=y[g, half][:, first : first + count, :],
+                )
+
+        def direct_clip(i):
+            clip(i // 2, 2 * (i % 2), 2, v_bank[i][:])
+
+        pooled = set()
+
+        def pool_weigh(q, first, count):
+            pooled.add((q, first))
+            weigh(nc.gpsimd, q, slice(0, POOL_COLS), first, count)
+
+        def warm(count):
+            bank = v_psum.tile([P, GROUP], F32, name="v_bank")
+            for n in range(count):
+                nc.tensor.matmul_mx(
+                    out=bank[:],
+                    lhsT=x_raw[0, 0][:, :P].bitcast(FP8X4),
+                    lhsT_scale=a_scale[2][:, 0, :P],
+                    rhs=x_raw[0, 0][:].bitcast(FP8X4),
+                    rhs_scale=a_scale[2][:, 0, :],
+                    start=True,
+                    stop=True,
+                )
+
+        def weigh_store(q, first, count):
+            weigh(nc.vector, q, slice(POOL_COLS if (q, first) in pooled else 0, STRIP), first, count)
+            store_y(q, first, count)
+
+        def round_y(q, first, count, eng):
+            strip, half = divmod(q, HALVES)
+            g, hh = divmod(strip, 2)
+            if (g, half) not in y_bf:
+                y_bf[g, half] = flow.tile([P, PACK, 2, STRIP], BF16, name="y_bf", bufs=4, align_bytes=64)
+            (nc.vector.tensor_copy if eng == "V" else nc.scalar.copy)(
+                out=y_bf[g, half][:, first : first + count, :, P * hh : P * (hh + 1)].rearrange(
+                    "p j u (m e) -> p u j m e", e=2
+                ),
+                in_=y_rows(q, first, count).rearrange("p j (m u e) -> p u j m e", u=2, e=2),
+            )
+
+        def transpose_y(g, half, first, count):
+            yt_bank[g, half, first] = t_psum.tile([P, count, 2, P], F32, name="t_bank")
+            for j in range(count):
                 for u in range(2):
-                    nc.tensor.transpose(yt_bank[g, pair][:, j, u, :], y_bf[g, pair][:, u, j, :].bitcast(F32), ident[:])
+                    nc.tensor.transpose(
+                        yt_bank[g, half, first][:, j, u, :], y_bf[g, half][:, first + j, u, :].bitcast(F32), ident[:]
+                    )
 
-        def unload_y(g, pair):
-            yt_bf[g, pair] = flow.tile([P, 2 * P * PACK], BF16, name="yt_bf", bufs=3, align_bytes=64)
-            nc.scalar.copy(
-                out=yt_bf[g, pair][:].bitcast(F32).rearrange("p (j r u) -> p j r u", j=2, u=2),
-                in_=yt_bank[g, pair][:].rearrange("p j u r -> p j r u"),
+        def unload_y(g, half, first, count, eng):
+            if (g, half) not in yt_bf:
+                yt_bf[g, half] = flow.tile([P, PACK, P * PACK], BF16, name="yt_bf", bufs=2, align_bytes=64)
+            (nc.vector.tensor_copy if eng == "V" else nc.scalar.copy)(
+                out=yt_bf[g, half][:, first : first + count, :].bitcast(F32).rearrange("p j (r u) -> p j r u", u=2),
+                in_=yt_bank[g, half, first][:].rearrange("p j u r -> p j r u"),
             )
 
-        def quantize_y(g, pair):
-            cols = slice(2 * P * pair, 2 * P * (pair + 1))
+        def quantize_y(g, half, first=0, count=4):
+            cols = slice(GROUP * half + P * first, GROUP * half + P * (first + count))
             nc.vector.quantize_mx(
-                out=y_code[g][:, cols].bitcast(FP8X4), scales=y_scale[g][:, cols], in_=yt_bf[g, pair][:]
+                out=y_code[g][:, cols].bitcast(FP8X4),
+                scales=y_scale[g][:, cols],
+                in_=yt_bf[g, half][:, first : first + count, :].rearrange("p j n -> p (j n)"),
             )
-            last_group = g == S_GROUPS - 1
-            if last_group or pair % 2 == 1:
-                first = pair if last_group else pair - 1
-                cols = slice(2 * P * first, 2 * P * (pair + 1))
-                words = out_1[g].rearrange("p m t -> p (m t)").bitcast(I32)
-                nc.sync.dma_start(out=words[:, cols], in_=y_code[g][:, cols])
-            if pair == PAIRS - 1:
+            words = out_1[g].rearrange("p m t -> p (m t)").bitcast(I32)
+            nc.sync.dma_start(out=words[:, cols], in_=y_code[g][:, cols])
+            done_cols[g] = done_cols.get(g, 0) + P * count
+            if done_cols[g] == PATCHES:
                 for quad in range(4):
-                    nc.sync.dma_start(
+                    (nc.scalar if g == S_GROUPS - 1 and quad % 2 else nc.sync).dma_start(
                         out=out_2[g, 4 * quad : 4 * quad + 4, :].bitcast(I32),
                         in_=y_scale[g][32 * quad : 32 * quad + 4, :].bitcast(I32),
                     )
 
-        transpose_at, unload_at, quantize_at = {}, {}, {}
-        for g in range(S_GROUPS):
-            for pair in range(PAIRS):
-                rounded = LAG + 3 + 2 * PAIRS * g + PAIRS
-                if g == S_GROUPS - 1:
-                    turned = rounded + pair
-                    unloaded = turned + 1
-                    done = unloaded
-                else:
-                    turned = rounded + (pair | 1) + 1
-                    unloaded = turned + 1 + pair % 2
-                    done = unloaded + 1
-                transpose_at.setdefault(turned, []).append((g, pair))
-                unload_at.setdefault(unloaded, []).append((g, pair))
-                quantize_at.setdefault(done, []).append((g, pair))
+        def completes(q):
+            strip, half = divmod(q, HALVES)
+            return (strip // 2, half) if 0 <= q < ROUNDS and strip % 2 == 1 else None
 
-        for step in range(max(quantize_at) + 1):
-            i = step - LAG
-            if step < UNITS:
-                interactions(step)
-            if 0 <= i < UNITS:
-                mix(i)
-            if 0 <= i - 1 < UNITS:
-                unload_mix(i - 1)
-            if 0 <= step - 1 < UNITS:
-                add_growth(step - 1)
-            if 0 <= i - 2 < UNITS:
-                weigh(i - 2)
-            if 0 <= step - 1 < UNITS and step % 2 == 0:
-                quantize_h((step - 1) // 4, (step - 1) // 2 % 2)
-            if 0 <= i - 1 < UNITS:
-                clip(i - 1)
-            if 0 <= i - 3 < UNITS:
-                round_y(i - 3)
-            if 0 <= i + 1 < PAIRS:
-                unload_dispersal(i + 1)
-                quantize_dispersal(i + 1)
-            for g, pair in unload_at.get(step, []):
-                unload_y(g, pair)
-            for g, pair in quantize_at.get(step, []):
-                quantize_y(g, pair)
-            if 0 <= i + 2 < PAIRS:
-                transpose_dispersal(i + 2)
-            for g, pair in transpose_at.get(step, []):
-                transpose_y(g, pair)
+        everything = slice(0, STRIP)
+        steps = {"s1": interactions, "add": add_growth, "qh": quantize_h, "od": order_dispersal, "td": transpose_dispersal, "ud": unload_dispersal, "qd": quantize_dispersal, "mix": mix, "um": unload_mix, "clip": clip, "dclip": direct_clip, "w": weigh_store, "gw": pool_weigh, "warm": warm, "late": late_loads, "ry": round_y, "ty": transpose_y, "uy": unload_y, "qy": quantize_y, "xw": order_x_words, "xs": order_x_scales}
+        for name, *args in STEPS:
+            steps[name](*args)

from contextlib import ExitStack

import concourse.mybir as mybir
from concourse.masks import make_identity

PATCHES, SPECIES = 1024, 1536
LOW, HIGH = -0.5, 1.5
FLOPS = 2 * PATCHES * SPECIES * SPECIES + 2 * PATCHES * PATCHES * SPECIES

F32 = mybir.dt.float32
BF16 = mybir.dt.bfloat16
I32 = mybir.dt.int32
U8 = mybir.dt.uint8
FP8X4 = mybir.dt.float8_e4m3fn_x4
FP4X4 = mybir.dt.float4_e2m1fn_x4
ALU = mybir.AluOpType

P = 128
PACK = 4
GROUP = P * PACK
S_GROUPS = SPECIES // GROUP
P_GROUPS = PATCHES // GROUP
STRIP = 256
STRIPS = SPECIES // STRIP
PAIRS = PATCHES // (2 * P)
UNITS = STRIPS * PAIRS
HALVES = PATCHES // GROUP
ROUNDS = STRIPS * HALVES
LAG = 2
RUN = 4
POOL_COLS = 80
LOADS = (("x", 0,), ("xs",), ("as", 0,), ("a", 0, 1,), ("d", 0,), ("x", 1,), ("g", 0, 0, 1,), ("d", 1,), ("g", 1, 0, 1,), ("a", 1, 1,), ("d", 2,), ("d", 3,), ("g", 0, 1, 1,), ("g", 1, 1, 1,), ("a", 2, 2,), ("h", 0, 2, 0,), ("as", 1,), ("h", 0, 2, 1,), ("g", 0, 2, 2,), ("as", 2,), ("g", 1, 2, 2,), ("a", 4, 2,), ("h", 2, 4, 0,), ("h", 2, 4, 1,), ("g", 0, 4, 2,), ("g", 1, 4, 2,))
STEPS = (("late",), ("xw", 0,), ("xs", 0, 2, 2,), ("od", 1, "N",), ("od", 0, "S",), ("xs", 0, 0, 2,), ("xs", 1, 0, 4,), ("xw", 1,), ("s1", 0,), ("add", 0,), ("td", 0,), ("ud", 0, 0, "S",), ("s1", 2,), ("add", 1,), ("ud", 0, 1, "S",), ("qh", 0, 0,), ("add", 2,), ("td", 1,), ("add", 3,), ("ud", 1, 1, "S",), ("qd", 0,), ("od", 2, "V",), ("ud", 1, 0, "S",), ("s1", 4,), ("qd", 1,), ("td", 2,), ("qh", 0, 1,), ("mix", 1,), ("ud", 2, 0, "V",), ("od", 3, "S",), ("ud", 2, 1, "S",), ("add", 4,), ("mix", 0,), ("add", 5,), ("qd", 2,), ("um", 0,), ("td", 3,), ("s1", 6,), ("ud", 3, 0, "S",), ("ud", 3, 1, "V",), ("qh", 1, 0,), ("um", 1,), ("qd", 3,), ("mix", 3,), ("clip", 0, 0, 4,), ("mix", 2,), ("um", 3,), ("add", 6,), ("add", 7,), ("gw", 0, 0, 4,), ("qh", 1, 1,), ("um", 2,), ("w", 0, 0, 4,), ("s1", 8,), ("mix", 5,), ("clip", 1, 0, 4,), ("gw", 1, 0, 4,), ("mix", 4,), ("ry", 0, 0, 4, "S",), ("um", 5,), ("add", 8,), ("add", 9,), ("w", 1, 0, 4,), ("qh", 2, 0,), ("um", 4,), ("ry", 1, 0, 4, "S",), ("s1", 10,), ("mix", 7,), ("clip", 2, 0, 4,), ("mix", 6,), ("um", 7,), ("add", 10,), ("add", 11,), ("gw", 2, 0, 4,), ("qh", 2, 1,), ("um", 6,), ("w", 2, 0, 4,), ("s1", 12,), ("mix", 9,), ("clip", 3, 0, 4,), ("gw", 3, 0, 4,), ("mix", 8,), ("ry", 2, 0, 4, "S",), ("um", 9,), ("add", 12,), ("add", 13,), ("w", 3, 0, 4,), ("qh", 3, 0,), ("um", 8,), ("ry", 3, 0, 4, "S",), ("s1", 14,), ("mix", 11,), ("clip", 4, 0, 4,), ("mix", 10,), ("um", 11,), ("add", 14,), ("add", 15,), ("gw", 4, 0, 4,), ("qh", 3, 1,), ("ty", 0, 0, 2, 2,), ("ty", 0, 0, 0, 2,), ("um", 10,), ("w", 4, 0, 4,), ("s1", 16,), ("uy", 0, 0, 2, 2, "S",), ("uy", 0, 0, 0, 2, "S",), ("mix", 13,), ("clip", 5, 0, 4,), ("gw", 5, 0, 4,), ("qy", 0, 0, 0, 4,), ("mix", 12,), ("ry", 4, 0, 4, "S",), ("um", 13,), ("add", 16,), ("add", 17,), ("w", 5, 0, 4,), ("qh", 4, 0,), ("um", 12,), ("ry", 5, 0, 4, "S",), ("s1", 18,), ("mix", 15,), ("clip", 6, 0, 4,), ("mix", 14,), ("um", 15,), ("add", 18,), ("add", 19,), ("gw", 6, 0, 4,), ("qh", 4, 1,), ("ty", 0, 1, 2, 2,), ("ty", 0, 1, 0, 2,), ("um", 14,), ("w", 6, 0, 4,), ("s1", 20,), ("uy", 0, 1, 2, 2, "S",), ("uy", 0, 1, 0, 2, "S",), ("mix", 17,), ("clip", 7, 0, 4,), ("gw", 7, 0, 4,), ("qy", 0, 1, 0, 4,), ("mix", 16,), ("ry", 6, 0, 4, "S",), ("um", 17,), ("add", 20,), ("add", 21,), ("w", 7, 0, 4,), ("qh", 5, 0,), ("um", 16,), ("ry", 7, 0, 4, "S",), ("s1", 22,), ("clip", 8, 0, 4,), ("mix", 18,), ("gw", 8, 0, 4,), ("add", 22,), ("um", 18,), ("mix", 19,), ("ty", 1, 0, 2, 2,), ("add", 23,), ("ty", 1, 1, 2, 2,), ("clip", 9, 0, 2,), ("um", 19,), ("qh", 5, 1,), ("mix", 20,), ("w", 8, 0, 4,), ("uy", 1, 0, 2, 2, "S",), ("clip", 9, 2, 2,), ("mix", 21,), ("ty", 1, 0, 0, 2,), ("uy", 1, 1, 2, 2, "S",), ("ry", 8, 0, 4, "S",), ("um", 21,), ("dclip", 20,), ("w", 9, 2, 2,), ("w", 10, 0, 2,), ("w", 9, 0, 2,), ("clip", 10, 2, 2,), ("mix", 22,), ("uy", 1, 0, 0, 2, "S",), ("qy", 1, 0, 0, 4,), ("ty", 1, 1, 0, 2,), ("mix", 23,), ("dclip", 22,), ("ry", 10, 0, 2, "S",), ("uy", 1, 1, 0, 2, "S",), ("ry", 9, 0, 2, "S",), ("w", 10, 2, 2,), ("ty", 2, 0, 0, 2,), ("w", 11, 0, 2,), ("qy", 1, 1, 0, 4,), ("uy", 2, 0, 0, 2, "S",), ("dclip", 23,), ("ry", 10, 2, 2, "S",), ("ry", 11, 0, 2, "S",), ("ry", 9, 2, 2, "S",), ("qy", 2, 0, 0, 2,), ("ty", 2, 0, 2, 2,), ("ty", 2, 1, 0, 2,), ("uy", 2, 0, 2, 2, "S",), ("w", 11, 3, 1,), ("w", 11, 2, 1,), ("ry", 11, 3, 1, "V",), ("uy", 2, 1, 0, 2, "S",), ("ty", 2, 1, 3, 1,), ("uy", 2, 1, 3, 1, "S",), ("ry", 11, 2, 1, "V",), ("qy", 2, 0, 2, 2,), ("ty", 2, 1, 2, 1,), ("qy", 2, 1, 0, 2,), ("uy", 2, 1, 2, 1, "V",), ("qy", 2, 1, 3, 1,), ("qy", 2, 1, 2, 1,))
EARLY = 4
WIDE_STORES = 1


def tile_dispersed_species_growth_h2_kernel(
    tc, x_words, x_scales, a_words, a_scales, growth, dispersal, habitat, out_0, out_1, out_2
):
    nc = tc.nc
    with ExitStack() as ctx:
        keep = ctx.enter_context(tc.tile_pool(name="keep", bufs=1))
        flow = ctx.enter_context(tc.tile_pool(name="flow", bufs=2))
        h_psum = ctx.enter_context(tc.psum_pool(name="h_psum", bufs=4))
        v_psum = ctx.enter_context(tc.psum_pool(name="v_psum", bufs=2))
        t_psum = ctx.enter_context(tc.psum_pool(name="t_psum", bufs=2))
        ctx.enter_context(tc.manual_schedule())

        def kept(name, shape, dtype):
            return keep.tile(shape, dtype, name=name, align_bytes=64)

        def load_scale_rows(plane, scales, cols):
            for quad in range(4):
                nc.sync.dma_start(
                    out=plane[32 * quad : 32 * quad + 4, :, :].bitcast(I32),
                    in_=scales[:, 4 * quad : 4 * quad + 4, cols].rearrange("g r n -> r g n").bitcast(I32),
                )

        x_scale_raw = kept("x_scale_raw", [P, S_GROUPS, PATCHES], U8)
        a_scale = [kept("a_scale_%d" % c, [P, S_GROUPS, GROUP], U8) for c in range(S_GROUPS)]
        ident = kept("ident", [P, P], F32)
        for plane in [x_scale_raw] + a_scale:
            nc.vector.memset(plane[:].bitcast(I32), 0)
        nc.vector.memset(ident[:], 0.0)
        make_identity(nc, ident[:], nomemset=True)

        x_raw, a_code, grow, disp, hab = {}, {}, {}, {}, {}

        def load_x(pg):
            for sg in range(S_GROUPS):
                x_raw[pg, sg] = kept("x_raw_%d_%d" % (pg, sg), [P, GROUP], I32)
                row = x_words[sg].rearrange("p n t -> p (n t)")
                nc.sync.dma_start(
                    out=x_raw[pg, sg][:], in_=row[:, PACK * GROUP * pg : PACK * GROUP * (pg + 1)].bitcast(I32)
                )

        def load_a(first_strip, strips):
            tile = kept("a_code_%d" % first_strip, [P, S_GROUPS, 2 * STRIP * strips], U8)
            cols = slice(2 * STRIP * first_strip, 2 * STRIP * (first_strip + strips))
            nc.sync.dma_start(
                out=tile[:].bitcast(I32), in_=a_words[:, :, cols].rearrange("g p n -> p g n").bitcast(I32)
            )
            for s in range(strips):
                a_code[first_strip + s] = tile[:, :, 2 * STRIP * s : 2 * STRIP * (s + 1)]

        def load_growth(pg, first_strip, strips):
            tile = kept("grow_%d_%d" % (pg, first_strip), [P, PACK, strips * STRIP], BF16)
            cols = slice(first_strip * STRIP, (first_strip + strips) * STRIP)
            nc.sync.dma_start(
                out=tile[:], in_=growth[GROUP * pg : GROUP * (pg + 1), cols].rearrange("(p t) s -> p t s", t=PACK)
            )
            for s in range(strips):
                grow[pg, first_strip + s] = tile[:, :, s * STRIP : (s + 1) * STRIP]

        def load_dispersal(pair):
            disp[pair] = kept("disp_%d" % pair, [P, 2, PATCHES], BF16)
            nc.sync.dma_start(
                out=disp[pair][:],
                in_=dispersal[2 * P * pair : 2 * P * (pair + 1), :].rearrange("(j p) k -> p j k", p=P),
            )

        def load_habitat(first_strip, strips, half):
            tile = kept("hab_%d_%d" % (first_strip, half), [P, PACK, strips * STRIP], BF16)
            cols = slice(first_strip * STRIP, (first_strip + strips) * STRIP)
            nc.sync.dma_start(
                out=tile[:],
                in_=habitat[GROUP * half : GROUP * (half + 1), cols].rearrange("(j p) s -> p j s", p=P),
            )
            for s in range(strips):
                hab[first_strip + s, half] = tile[:, :, s * STRIP : (s + 1) * STRIP]

        loaders = {"x": load_x, "xs": lambda: load_scale_rows(x_scale_raw, x_scales, slice(0, PATCHES)), "as": lambda c: load_scale_rows(a_scale[c], a_scales, slice(c * GROUP, (c + 1) * GROUP)), "a": load_a, "g": load_growth, "d": load_dispersal, "h": load_habitat}
        for name, *args in LOADS[:EARLY]:
            loaders[name](*args)

        def late_loads():
            for name, *args in LOADS[EARLY:]:
                loaders[name](*args)

        x_code, x_scale = {}, {}

        def order_x_words(pg):
            for sg in range(S_GROUPS):
                x_code[pg, sg] = kept("x_code_%d_%d" % (pg, sg), [P, GROUP], I32)
                nc.vector.tensor_copy(
                    out=x_code[pg, sg][:].rearrange("p (t m) -> p m t", t=PACK),
                    in_=x_raw[pg, sg][:].rearrange("p (m t) -> p m t", t=PACK),
                )

        def order_x_scales(pg, first_t, count):
            tile = kept("x_scale_%d_%d" % (pg, first_t), [P, count, S_GROUPS, P], U8)
            raw = x_scale_raw[:, :, GROUP * pg : GROUP * (pg + 1)].rearrange("p g (m t) -> p t g m", t=PACK)
            nc.vector.tensor_copy(out=tile[:], in_=raw[:, first_t : first_t + count])
            for t in range(count):
                x_scale[pg, first_t + t] = tile[:, t]


        h_bank, h_bf, h_code, h_scale = {}, {}, {}, {}
        d_words, d_bank, d_bf, d_code, d_scale = {}, {}, {}, {}, {}
        v_bank, y, y_bf = {}, {}, {}
        yt_bank, yt_bf, done_cols = {}, {}, {}
        y_code = [kept("y_code_%d" % g, [P, PATCHES], I32) for g in range(S_GROUPS)]
        y_scale = [kept("y_scale_%d" % g, [P, PATCHES], U8) for g in range(S_GROUPS)]

        def interactions(k):
            strip, pg = k // 4, k // 2 % 2
            c, first = divmod(strip * STRIP, GROUP)
            for b in range(2):
                h_bank[k + b] = h_psum.tile([P, PACK, P], F32, name="h_bank")
            for t in range(PACK):
                cols = slice(P * t, P * (t + 1))
                for sg in range(S_GROUPS):
                    for b in range(2):
                        nc.tensor.matmul_mx(
                            out=h_bank[k + b][:, t, :],
                            lhsT=x_code[pg, sg][:, cols].bitcast(FP8X4),
                            lhsT_scale=x_scale[pg, t][:, sg, :],
                            rhs=a_code[strip][:, sg, 2 * P * b : 2 * P * (b + 1)].bitcast(FP4X4),
                            rhs_scale=a_scale[c][:, sg, first + P * b : first + P * (b + 1)],
                            start=(sg == 0),
                            stop=(sg == S_GROUPS - 1),
                        )

        def add_growth(k):
            strip, pg, b = k // 4, k // 2 % 2, k % 2
            if b == 0:
                h_bf[strip, pg] = flow.tile([P, STRIP, PACK], BF16, name="h_bf", bufs=3, align_bytes=64)
            nc.vector.tensor_tensor(
                out=h_bf[strip, pg][:, P * b : P * (b + 1), :].rearrange("p (c i) t -> p c t i", i=RUN),
                in0=h_bank[k][:].rearrange("p t (c i) -> p c t i", i=RUN),
                in1=grow[pg, strip][:, :, P * b : P * (b + 1)].rearrange("p t (c i) -> p c t i", i=RUN),
                op=ALU.add,
            )

        def quantize_h(strip, pg):
            h_code[strip, pg] = kept("h_code_%d_%d" % (strip, pg), [P, STRIP], I32)
            h_scale[strip, pg] = kept("h_scale_%d_%d" % (strip, pg), [P, STRIP], U8)
            nc.vector.quantize_mx(
                out=h_code[strip, pg][:].bitcast(FP8X4),
                scales=h_scale[strip, pg][:],
                in_=h_bf[strip, pg][:].rearrange("p n t -> p (n t)"),
            )

        def order_dispersal(pair, eng):
            if eng == "N":
                return
            d_words[pair] = flow.tile([P, 2 * P_GROUPS, 2, P], F32, name="d_words", bufs=2, align_bytes=64)
            words = disp[pair][:].rearrange("p j k -> p (j k)").bitcast(F32)
            (nc.vector.tensor_copy if eng == "V" else nc.scalar.copy)(out=d_words[pair][:], in_=words.rearrange("p (a m u) -> p a u m", m=P, u=2))

        def transpose_dispersal(pair):
            for j in range(2):
                d_bank[pair, j] = t_psum.tile([P, P_GROUPS, 2, P], F32, name="t_bank")
                for pg in range(P_GROUPS):
                    for u in range(2):
                        nc.tensor.transpose(
                            d_bank[pair, j][:, pg, u, :], d_words[pair][:, P_GROUPS * j + pg, u, :] if pair in d_words else disp[pair][:, j, :].bitcast(F32)[:, 2 * P * pg + u : 2 * P * (pg + 1) : 2], ident[:]
                        )

        def unload_dispersal(pair, j, eng):
            if pair not in d_bf:
                d_bf[pair] = flow.tile([P, 2, P_GROUPS * P * PACK], BF16, name="yt_bf", bufs=2, align_bytes=64)
            (nc.vector.tensor_copy if eng == "V" else nc.scalar.copy)(
                out=d_bf[pair][:, j, :].bitcast(F32).rearrange("p (g r u) -> p g r u", g=P_GROUPS, u=2),
                in_=d_bank[pair, j][:].rearrange("p g u r -> p g r u"),
            )

        def quantize_dispersal(pair):
            d_code[pair] = kept("d_code_%d" % pair, [P, 2 * P_GROUPS * P], I32)
            d_scale[pair] = kept("d_scale_%d" % pair, [P, 2 * P_GROUPS * P], U8)
            nc.vector.quantize_mx(
                out=d_code[pair][:].bitcast(FP8X4),
                scales=d_scale[pair][:],
                in_=d_bf[pair][:].rearrange("p j n -> p (j n)"),
            )

        def mix(i):
            strip, pair = divmod(i, PAIRS)
            v_bank[i] = v_psum.tile([P, 2, STRIP], F32, name="v_bank")
            for j in range(2):
                for pg in range(P_GROUPS):
                    cols = slice(P * (P_GROUPS * j + pg), P * (P_GROUPS * j + pg + 1))
                    nc.tensor.matmul_mx(
                        out=v_bank[i][:, j, :],
                        lhsT=d_code[pair][:, cols].bitcast(FP8X4),
                        lhsT_scale=d_scale[pair][:, cols],
                        rhs=h_code[strip, pg][:].bitcast(FP8X4),
                        rhs_scale=h_scale[strip, pg][:],
                        start=(pg == 0),
                        stop=(pg == P_GROUPS - 1),
                    )

        def y_rows(q, first, count):
            strip, half = divmod(q, HALVES)
            g, hh = divmod(strip, 2)
            if g >= WIDE_STORES:
                if q not in y:
                    y[q] = kept("y_%d" % q, [P, PACK, STRIP], F32)
                return y[q][:, first : first + count, :]
            if (g, half) not in y:
                y[g, half] = kept("y_%d_%d" % (g, half), [P, PACK, GROUP], F32)
            return y[g, half][:, first : first + count, STRIP * hh : STRIP * (hh + 1)]

        def unload_mix(i):
            nc.scalar.copy(out=y_rows(i // 2, 2 * (i % 2), 2), in_=v_bank[i][:])

        def clip(q, first=0, count=4, source=None):
            rows = y_rows(q, first, count)
            nc.vector.tensor_scalar(
                out=rows, in0=rows if source is None else source, scalar1=LOW, scalar2=HIGH, op0=ALU.max, op1=ALU.min
            )

        def weigh(engine, q, cols, first=0, count=4):
            strip, half = divmod(q, HALVES)
            rows = y_rows(q, first, count)[:, :, cols]
            engine.tensor_tensor(out=rows, in0=rows, in1=hab[strip, half][:, first : first + count, cols], op=ALU.mult)

        def store_y(q, first=0, count=4):
            strip, half = divmod(q, HALVES)
            g, hh = divmod(strip, 2)
            rows = slice(GROUP * half + P * first, GROUP * half + P * (first + count))
            if g >= WIDE_STORES:
                nc.sync.dma_start(
                    out=out_0[rows, STRIP * strip : STRIP * (strip + 1)].rearrange("(j p) s -> p j s", p=P),
                    in_=y_rows(q, first, count),
                )
            elif hh == 1:
                nc.sync.dma_start(
                    out=out_0[rows, GROUP * g : GROUP * (g + 1)].rearrange("(j p) s -> p j s", p=P),
                    in_=y[g, half][:, first : first + count, :],
                )

        def direct_clip(i):
            clip(i // 2, 2 * (i % 2), 2, v_bank[i][:])

        pooled = set()

        def pool_weigh(q, first, count):
            pooled.add((q, first))
            weigh(nc.gpsimd, q, slice(0, POOL_COLS), first, count)

        def warm(count):
            bank = v_psum.tile([P, GROUP], F32, name="v_bank")
            for n in range(count):
                nc.tensor.matmul_mx(
                    out=bank[:],
                    lhsT=x_raw[0, 0][:, :P].bitcast(FP8X4),
                    lhsT_scale=a_scale[2][:, 0, :P],
                    rhs=x_raw[0, 0][:].bitcast(FP8X4),
                    rhs_scale=a_scale[2][:, 0, :],
                    start=True,
                    stop=True,
                )

        def weigh_store(q, first, count):
            weigh(nc.vector, q, slice(POOL_COLS if (q, first) in pooled else 0, STRIP), first, count)
            store_y(q, first, count)

        def round_y(q, first, count, eng):
            strip, half = divmod(q, HALVES)
            g, hh = divmod(strip, 2)
            if (g, half) not in y_bf:
                y_bf[g, half] = flow.tile([P, PACK, 2, STRIP], BF16, name="y_bf", bufs=4, align_bytes=64)
            (nc.vector.tensor_copy if eng == "V" else nc.scalar.copy)(
                out=y_bf[g, half][:, first : first + count, :, P * hh : P * (hh + 1)].rearrange(
                    "p j u (m e) -> p u j m e", e=2
                ),
                in_=y_rows(q, first, count).rearrange("p j (m u e) -> p u j m e", u=2, e=2),
            )

        def transpose_y(g, half, first, count):
            yt_bank[g, half, first] = t_psum.tile([P, count, 2, P], F32, name="t_bank")
            for j in range(count):
                for u in range(2):
                    nc.tensor.transpose(
                        yt_bank[g, half, first][:, j, u, :], y_bf[g, half][:, first + j, u, :].bitcast(F32), ident[:]
                    )

        def unload_y(g, half, first, count, eng):
            if (g, half) not in yt_bf:
                yt_bf[g, half] = flow.tile([P, PACK, P * PACK], BF16, name="yt_bf", bufs=2, align_bytes=64)
            (nc.vector.tensor_copy if eng == "V" else nc.scalar.copy)(
                out=yt_bf[g, half][:, first : first + count, :].bitcast(F32).rearrange("p j (r u) -> p j r u", u=2),
                in_=yt_bank[g, half, first][:].rearrange("p j u r -> p j r u"),
            )

        def quantize_y(g, half, first=0, count=4):
            cols = slice(GROUP * half + P * first, GROUP * half + P * (first + count))
            nc.vector.quantize_mx(
                out=y_code[g][:, cols].bitcast(FP8X4),
                scales=y_scale[g][:, cols],
                in_=yt_bf[g, half][:, first : first + count, :].rearrange("p j n -> p (j n)"),
            )
            words = out_1[g].rearrange("p m t -> p (m t)").bitcast(I32)
            nc.sync.dma_start(out=words[:, cols], in_=y_code[g][:, cols])
            done_cols[g] = done_cols.get(g, 0) + P * count
            if done_cols[g] == PATCHES:
                for quad in range(4):
                    (nc.scalar if g == S_GROUPS - 1 and quad % 2 else nc.sync).dma_start(
                        out=out_2[g, 4 * quad : 4 * quad + 4, :].bitcast(I32),
                        in_=y_scale[g][32 * quad : 32 * quad + 4, :].bitcast(I32),
                    )

        def completes(q):
            strip, half = divmod(q, HALVES)
            return (strip // 2, half) if 0 <= q < ROUNDS and strip % 2 == 1 else None

        everything = slice(0, STRIP)
        steps = {"s1": interactions, "add": add_growth, "qh": quantize_h, "od": order_dispersal, "td": transpose_dispersal, "ud": unload_dispersal, "qd": quantize_dispersal, "mix": mix, "um": unload_mix, "clip": clip, "dclip": direct_clip, "w": weigh_store, "gw": pool_weigh, "warm": warm, "late": late_loads, "ry": round_y, "ty": transpose_y, "uy": unload_y, "qy": quantize_y, "xw": order_x_words, "xs": order_x_scales}
        for name, *args in STEPS:
            steps[name](*args)
